import numpy as np
import ml_dtypes


def mxq(x, axis, fmt="e4m3"):
    dtype, down = {"e4m3": (ml_dtypes.float8_e4m3fn, 7), "e5m2": (ml_dtypes.float8_e5m2, 14)}[fmt]
    v = np.moveaxis(np.asarray(x, np.float32).astype(ml_dtypes.bfloat16).astype(np.float64), axis, -1)
    blocks = v.reshape(v.shape[:-1] + (-1, 32))
    amax = np.abs(blocks).max(-1, keepdims=True)
    byte = np.maximum(np.where(amax > 0, np.frexp(amax)[1] - 1 + 127, 0) - down, 1)
    scale = np.exp2(byte - 127.0)
    codes = (blocks / scale).astype(np.float32).astype(dtype).astype(np.float64)
    return np.moveaxis((codes * scale).reshape(v.shape), -1, axis)


WIDE = False


def mx_kscale(k):
    if not WIDE:
        return np.ones(k)
    levels = np.array([30, -30])
    if k % 512:
        return np.exp2(np.random.permutation(np.resize(levels, k // 32))).repeat(32)
    a = np.empty((k // 512, 16))
    for p in range(k // 512):
        a[p, :8] = np.random.permutation(np.resize(levels, 8))
        for g in range(8):
            far = levels[np.abs(levels - a[p, g]) >= 10]
            a[p, g + 8] = far[np.random.randint(len(far))]
    return np.exp2(a.ravel()).repeat(32)


def f64(x):
    return np.asarray(x).astype(np.float64)


def striped(idx):
    return np.tile(np.asarray(idx).reshape(-1, 16).T, (8, 1)).astype(np.uint16)


def unstriped(offs):
    return offs[:16].T.reshape(-1).astype(np.int64)


E2M1 = np.array([0.0, 0.5, 1.0, 1.5, 2.0, 3.0, 4.0, 6.0, -0.0, -0.5, -1.0, -1.5, -2.0, -3.0, -4.0, -6.0])


def pack_weight(w, fmt):
    k, n = w.shape
    w = f64(np.asarray(w, np.float32).astype(ml_dtypes.bfloat16)).reshape(k // 32, 32, n)
    amax = np.abs(w).max(1)
    if fmt in ("e4m3", "e5m2"):
        byte = np.frexp(amax)[1] - 1 + 127 - (7 if fmt == "e4m3" else 14)
    else:
        mant, ex = np.frexp(amax / 6.0)
        byte = np.where(mant > 0.5, ex, ex - 1) + 127
    byte = np.clip(np.where(amax > 0, byte, 1), 1, 254)
    scaled = (w * np.exp2(127.0 - byte)[:, None, :]).reshape(k, n).astype(np.float32)
    by_word = np.ascontiguousarray(scaled.reshape(k // 512, 128, 4, n).transpose(0, 1, 3, 2))
    if fmt in ("e4m3", "e5m2"):
        words = by_word.astype(ml_dtypes.float8_e4m3fn if fmt == "e4m3" else ml_dtypes.float8_e5m2).view(np.uint8)
    else:
        c = by_word.astype(ml_dtypes.float4_e2m1fn).view(np.uint8) & 0xF
        words = (c[..., 0::2] | (c[..., 1::2] << 4)).reshape(k // 512, 128, 2 * n)
    return np.ascontiguousarray(words), np.ascontiguousarray(byte.astype(np.uint8).reshape(k // 512, 16, n))


def unpack_weight(words, scales, fmt):
    g, _, n = scales.shape
    words = np.ascontiguousarray(words).reshape(g, 128, n, -1)
    if fmt in ("e4m3", "e5m2"):
        vals = words.view(ml_dtypes.float8_e4m3fn if fmt == "e4m3" else ml_dtypes.float8_e5m2).astype(np.float64)
    else:
        nib = np.empty((g, 128, n, 4), np.uint8)
        nib[..., 0::2] = words & 0xF
        nib[..., 1::2] = words >> 4
        vals = E2M1[nib]
    vals = vals * np.repeat(np.exp2(scales.astype(np.float64) - 127.0), 8, axis=1)[..., None]
    return vals.transpose(0, 1, 3, 2).reshape(g * 512, n)


K, T, J, R, N = 1024, 1024, 256, 512, 256


def setup_inputs():
    n = np.random.standard_normal
    idx = np.random.permutation(T)[:J]
    fk = mx_kscale(K)
    fr = mx_kscale(R)
    wp = pack_weight(n((K, R)) * 1 / np.sqrt(K) * fk[:, None] * fr, "e2m1")
    wbp = pack_weight(n((R, N)) * 1 / np.sqrt(R) / fr[:, None], "e5m2")
    return {
        "xf": (n((K, T))).astype(np.float32),
        "ow": (n((K, J)) * 0.7).astype(np.float32),
        "fk": (np.random.uniform(0.5, 2.0, (K, 1)) / fk[:, None]).astype(np.float32),
        "w_words": wp[0],
        "w_scales": wp[1],
        "wb_words": wbp[0],
        "wb_scales": wbp[1],
        "rs": (1.0 * n((J, N))).astype(np.float32),
        "offs": striped(idx),
    }


def reference(xf, ow, fk, w_words, w_scales, wb_words, wb_scales, rs, offs):
    idx = unstriped(offs)
    wu = unpack_weight(w_words, w_scales, "e2m1")
    wbu = unpack_weight(wb_words, wb_scales, "e5m2")
    u = (f64(xf)[:, idx] - f64(ow)) * f64(fk)
    uq = mxq(u, 0, "e4m3")
    a = wu.T @ uq
    pk1 = np.max(a, axis=1, keepdims=True)
    hid = np.maximum(a - 0.4 * pk1, 0.0)
    hidq = mxq(hid, 0, "e5m2")
    p = hidq.T @ wbu
    mn = np.mean(np.abs(p), axis=1, keepdims=True)
    y = np.maximum(p - mn, 0.0) - 0.3 * f64(rs)
    return y

@@ -1,0 +1,204 @@
+from contextlib import ExitStack
+
+import concourse.mybir as mybir
+
+K, T, J, R, N = 1024, 1024, 256, 512, 256
+FLOPS = 2 * K * R * J + 2 * R * J * N
+
+F32 = mybir.dt.float32
+BF16 = mybir.dt.bfloat16
+I32 = mybir.dt.int32
+U32 = mybir.dt.uint32
+U16 = mybir.dt.uint16
+U8 = mybir.dt.uint8
+E4M3X4 = mybir.dt.float8_e4m3fn_x4
+E5M2X4 = mybir.dt.float8_e5m2_x4
+E2M1X4 = mybir.dt.float4_e2m1fn_x4
+ALU = mybir.AluOpType
+ACT = mybir.ActivationFunctionType
+AXIS_X = mybir.AxisListType.X
+
+P = 128
+PACK = 4
+PASSES = K // (P * PACK)
+HALF = J // 2
+LIST_COL = 16
+
+
+def tile_list_offsetpicks_peakgated_rowabove_kernel(tc, xf, ow, fk, w_words, w_scales, wb_words, wb_scales, rs, offs, out):
+    nc = tc.nc
+    with ExitStack() as ctx:
+        keep = ctx.enter_context(tc.tile_pool(name="keep", bufs=1))
+        psum = ctx.enter_context(tc.psum_pool(name="psum", bufs=1))
+
+        offsets = keep.tile([P, J // LIST_COL], U16, name="offsets")
+        tokens = [[keep.tile([P, T], F32, name="tokens_%d_%d" % (z, t)) for t in range(PACK)] for z in range(PASSES)]
+        own = [keep.tile([P, PACK, J], F32, name="own_%d" % z) for z in range(PASSES)]
+        factor = keep.tile([P, PASSES, PACK], F32, name="factor")
+        w_raw = keep.tile([P, PASSES, R // 2], I32, name="w_raw")
+        w_codes = keep.tile([P, PASSES, R], U16, name="w_codes", align_bytes=64)
+        ws_raw = keep.tile([P, PASSES, R], U8, name="ws_raw")
+        w_plane = keep.tile([P, PASSES, R], U8, name="w_plane", align_bytes=64)
+        wb_codes = keep.tile([P, N], I32, name="wb_codes", align_bytes=64)
+        wb_plane = keep.tile([P, N], U8, name="wb_plane", align_bytes=64)
+        resid = keep.tile([P, 2, N], F32, name="resid")
+
+        nc.vector.memset(ws_raw[:].bitcast(I32), 0)
+        nc.vector.memset(wb_plane[:].bitcast(I32), 0)
+
+        xf_rows = xf.rearrange("(z p t) c -> z t p c", z=PASSES, t=PACK)
+        ow_rows = ow.rearrange("(z p t) j -> z p t j", z=PASSES, t=PACK)
+
+        def load_tokens(z, t):
+            nc.sync.dma_start(out=tokens[z][t][:], in_=xf_rows[z, t])
+
+        def load_w_scale_rows(q):
+            nc.sync.dma_start(
+                out=ws_raw[32 * q : 32 * q + 4].bitcast(I32),
+                in_=w_scales[:, 4 * q : 4 * q + 4, :].rearrange("z q c -> q z c").bitcast(I32),
+            )
+
+        load_tokens(0, 0)
+        nc.sync.dma_start(out=own[0][:], in_=ow_rows[0])
+        nc.sync.dma_start(offsets[:], offs)
+        nc.sync.dma_start(out=factor[:], in_=fk.rearrange("(z p t) o -> p z (t o)", z=PASSES, t=PACK))
+        load_tokens(0, 1)
+        nc.sync.dma_start(out=w_raw[:], in_=w_words.rearrange("z p c -> p z c").bitcast(I32))
+        load_w_scale_rows(0)
+        load_w_scale_rows(1)
+        load_tokens(0, 2)
+        load_w_scale_rows(2)
+        load_w_scale_rows(3)
+        load_tokens(0, 3)
+        nc.sync.dma_start(out=own[1][:], in_=ow_rows[1])
+        for t in range(PACK):
+            load_tokens(1, t)
+        for q in range(4):
+            nc.sync.dma_start(
+                out=wb_plane[32 * q : 32 * q + 4].bitcast(I32),
+                in_=wb_scales[0, 4 * q : 4 * q + 4, :].bitcast(I32),
+            )
+        nc.sync.dma_start(out=wb_codes[:], in_=wb_words[0].rearrange("p n t -> p (n t)").bitcast(I32))
+        nc.sync.dma_start(out=resid[:], in_=rs.rearrange("(h p) n -> p h n", h=2))
+
+        diff = [[keep.tile([P, J], F32, name="diff_%d_%d" % (z, t)) for t in range(PACK)] for z in range(PASSES)]
+        u = [keep.tile([P, J, PACK], BF16, name="u_%d" % z, align_bytes=64) for z in range(PASSES)]
+        u_codes = [keep.tile([P, J], U32, name="u_codes_%d" % z, align_bytes=64) for z in range(PASSES)]
+        u_plane = [keep.tile([P, J], U8, name="u_plane_%d" % z, align_bytes=64) for z in range(PASSES)]
+        first = [psum.tile([P, J], F32, name="first_%d" % t) for t in range(PACK)]
+        second = [psum.tile([P, N], F32, name="second_%d" % h) for h in range(2)]
+
+        def gather(z, t, j0, j1):
+            window = tokens[z][t][:].indirect(offsets[:, j0 // LIST_COL : j1 // LIST_COL])
+            nc.vector.tensor_tensor(diff[z][t][:, j0:j1], window, own[z][:, t, j0:j1], ALU.subtract)
+
+        def scale(z, t, j0, j1):
+            if t < 2:
+                nc.scalar.activation(u[z][:, j0:j1, t], diff[z][t][:, j0:j1], ACT.Copy, scale=factor[:, z, t : t + 1])
+            else:
+                nc.vector.tensor_scalar(u[z][:, j0:j1, t], diff[z][t][:, j0:j1], factor[:, z, t : t + 1], None, ALU.mult)
+
+        def quantize_u(z, j0, j1):
+            nc.vector.quantize_mx(
+                out=u_codes[z][:, j0:j1].bitcast(E4M3X4),
+                scales=u_plane[z][:, j0:j1],
+                in_=u[z][:, j0:j1, :].rearrange("p j t -> p (j t)"),
+            )
+
+        def first_product(z, t, j0, j1):
+            nc.tensor.matmul_mx(
+                out=first[t][:, j0:j1],
+                lhsT=w_codes[:, z, P * t : P * (t + 1)].bitcast(E2M1X4),
+                lhsT_scale=w_plane[:, z, P * t : P * (t + 1)],
+                rhs=u_codes[z][:, j0:j1].bitcast(E4M3X4),
+                rhs_scale=u_plane[z][:, j0:j1],
+                start=(z == 0),
+                stop=(z == PASSES - 1 and j1 == J),
+            )
+
+        def deal_words(z):
+            nc.vector.tensor_copy(
+                w_codes[:, z, :].rearrange("p (t c i) -> p c t i", t=PACK, i=8),
+                w_raw[:, z, :].bitcast(U16).rearrange("p (c i t) -> p c t i", t=PACK, i=8),
+            )
+
+        def deal_scales(z):
+            nc.vector.tensor_copy(
+                w_plane[:, z, :].rearrange("p (t c i) -> p c t i", t=PACK, i=16),
+                ws_raw[:, z, :].rearrange("p (c i t) -> p c t i", t=PACK, i=16),
+            )
+
+        for t in range(PACK):
+            gather(0, t, 0, J)
+            scale(0, t, 0, J)
+            if t == 1:
+                deal_words(0)
+                deal_words(1)
+            if t == 2:
+                deal_scales(0)
+        quantize_u(0, 0, J)
+        deal_scales(1)
+        for t in range(PACK):
+            first_product(0, t, 0, J)
+
+        for t in range(PACK - 1):
+            gather(1, t, 0, J)
+            scale(1, t, 0, J)
+        halves = [(0, HALF), (HALF, J)]
+        for step in (gather, scale):
+            for j0, j1 in halves:
+                step(1, PACK - 1, j0, j1)
+        for j0, j1 in halves:
+            quantize_u(1, j0, j1)
+        for t0 in (0, 2):
+            for j0, j1 in halves:
+                for t in (t0, t0 + 1):
+                    first_product(1, t, j0, j1)
+
+        neg_peak = [keep.tile([P, 1], F32, name="neg_peak_%d" % t) for t in range(PACK)]
+        above = keep.tile([P, PACK, J], F32, name="above")
+        hid = keep.tile([P, J, PACK], BF16, name="hid", align_bytes=64)
+        hid_codes = keep.tile([P, J], U32, name="hid_codes", align_bytes=64)
+        hid_plane = keep.tile([P, J], U8, name="hid_plane", align_bytes=64)
+
+        for t in range(PACK):
+            nc.vector.tensor_reduce(neg_peak[t][:], first[t][:], AXIS_X, ALU.max, negate=True)
+            for j0, j1 in (halves if t == PACK - 1 else [(0, J)]):
+                nc.scalar.activation(above[:, t, j0:j1], first[t][:, j0:j1], ACT.Relu, bias=neg_peak[t][:], scale=2.5)
+
+        def weave(t0, j0, j1):
+            nc.vector.tensor_scalar(
+                hid[:, j0:j1, t0 : t0 + 2], above[:, t0 : t0 + 2, j0:j1].rearrange("p t j -> p j t"), 0.4, None, ALU.mult
+            )
+
+        weave(0, 0, J)
+        for j0, j1 in halves:
+            weave(2, j0, j1)
+        for j0, j1 in halves:
+            nc.vector.quantize_mx(
+                out=hid_codes[:, j0:j1].bitcast(E5M2X4),
+                scales=hid_plane[:, j0:j1],
+                in_=hid[:, j0:j1, :].rearrange("p j t -> p (j t)"),
+            )
+        for h, (j0, j1) in enumerate(halves):
+            nc.tensor.matmul_mx(
+                out=second[h][:],
+                lhsT=hid_codes[:, j0:j1].bitcast(E5M2X4),
+                lhsT_scale=hid_plane[:, j0:j1],
+                rhs=wb_codes[:].bitcast(E5M2X4),
+                rhs_scale=wb_plane[:],
+                start=True,
+                stop=True,
+            )
+
+        magnitude = [keep.tile([P, N], BF16, name="magnitude_%d" % h) for h in range(2)]
+        mean = [keep.tile([P, 1], F32, name="mean_%d" % h) for h in range(2)]
+        kept = [keep.tile([P, N], F32, name="kept_%d" % h) for h in range(2)]
+        result = [keep.tile([P, N], F32, name="result_%d" % h) for h in range(2)]
+        for h in range(2):
+            nc.scalar.activation(magnitude[h][:], second[h][:], ACT.Abs, scale=1.0 / N, accum_out=mean[h][:])
+        for h in range(2):
+            nc.vector.tensor_scalar(kept[h][:], second[h][:], mean[h][:], 0.0, ALU.subtract, ALU.max)
+        for h in range(2):
+            nc.vector.scalar_tensor_tensor(result[h][:], resid[:, h, :], -0.3, kept[h][:], ALU.mult, ALU.add)
+            nc.sync.dma_start(out=out[HALF * h : HALF * (h + 1), :], in_=result[h][:])

@@ -1,6 +1,7 @@
 from contextlib import ExitStack
 
 import concourse.mybir as mybir
+from concourse.masks import make_identity
 
 K, T, J, R, N = 1024, 1024, 256, 512, 256
 FLOPS = 2 * K * R * J + 2 * R * J * N
@@ -43,8 +44,12 @@ def tile_list_offsetpicks_peakgated_rowabove_kernel(tc, xf, ow, fk, w_words, w_s
         wb_plane = keep.tile([P, N], U8, name="wb_plane", align_bytes=64)
         resid = keep.tile([P, 2, N], F32, name="resid")
 
-        nc.vector.memset(ws_raw[:].bitcast(I32), 0)
-        nc.vector.memset(wb_plane[:].bitcast(I32), 0)
+        factor_rows = keep.tile([P, P * PACK], F32, name="factor_rows")
+        identity = keep.tile([P, P], F32, name="identity")
+        nc.gpsimd.memset(factor_rows[:], 0.0)
+        nc.gpsimd.memset(ws_raw[:].bitcast(I32), 0)
+        make_identity(nc, identity[:])
+        nc.gpsimd.memset(wb_plane[:].bitcast(I32), 0)
 
         xf_rows = xf.rearrange("(z p t) c -> z t p c", z=PASSES, t=PACK)
         ow_rows = ow.rearrange("(z p t) j -> z p t j", z=PASSES, t=PACK)
@@ -59,11 +64,11 @@ def tile_list_offsetpicks_peakgated_rowabove_kernel(tc, xf, ow, fk, w_words, w_s
             )
 
         load_tokens(0, 0)
-        nc.sync.dma_start(out=own[0][:], in_=ow_rows[0])
         nc.sync.dma_start(offsets[:], offs)
-        nc.sync.dma_start(out=factor[:], in_=fk.rearrange("(z p t) o -> p z (t o)", z=PASSES, t=PACK))
-        load_tokens(0, 1)
+        nc.sync.dma_start(out=own[0][:], in_=ow_rows[0])
+        nc.sync.dma_start(out=factor_rows[0:PASSES, :], in_=fk.rearrange("(z c) o -> z (c o)", z=PASSES))
         nc.sync.dma_start(out=w_raw[:], in_=w_words.rearrange("z p c -> p z c").bitcast(I32))
+        load_tokens(0, 1)
         load_w_scale_rows(0)
         load_w_scale_rows(1)
         load_tokens(0, 2)
@@ -81,6 +86,11 @@ def tile_list_offsetpicks_peakgated_rowabove_kernel(tc, xf, ow, fk, w_words, w_s
         nc.sync.dma_start(out=wb_codes[:], in_=wb_words[0].rearrange("p n t -> p (n t)").bitcast(I32))
         nc.sync.dma_start(out=resid[:], in_=rs.rearrange("(h p) n -> p h n", h=2))
 
+        turned = psum.tile([P, PACK, P], F32, name="turned")
+        for t in range(PACK):
+            nc.tensor.transpose(turned[:, t, :], factor_rows[:, t :: PACK], identity[:])
+        nc.scalar.copy(factor[:], turned[:, :, 0:PASSES].rearrange("p t z -> p z t"))
+
         diff = [[keep.tile([P, J], F32, name="diff_%d_%d" % (z, t)) for t in range(PACK)] for z in range(PASSES)]
         u = [keep.tile([P, J, PACK], BF16, name="u_%d" % z, align_bytes=64) for z in range(PASSES)]
         u_codes = [keep.tile([P, J], U32, name="u_codes_%d" % z, align_bytes=64) for z in range(PASSES)]
@@ -93,7 +103,7 @@ def tile_list_offsetpicks_peakgated_rowabove_kernel(tc, xf, ow, fk, w_words, w_s
             nc.vector.tensor_tensor(diff[z][t][:, j0:j1], window, own[z][:, t, j0:j1], ALU.subtract)
 
         def scale(z, t, j0, j1):
-            if t < 2:
+            if z == 0 or t < 2:
                 nc.scalar.activation(u[z][:, j0:j1, t], diff[z][t][:, j0:j1], ACT.Copy, scale=factor[:, z, t : t + 1])
             else:
                 nc.vector.tensor_scalar(u[z][:, j0:j1, t], diff[z][t][:, j0:j1], factor[:, z, t : t + 1], None, ALU.mult)
@@ -131,13 +141,9 @@ def tile_list_offsetpicks_peakgated_rowabove_kernel(tc, xf, ow, fk, w_words, w_s
         for t in range(PACK):
             gather(0, t, 0, J)
             scale(0, t, 0, J)
-            if t == 1:
-                deal_words(0)
-                deal_words(1)
-            if t == 2:
-                deal_scales(0)
+            deal = deal_words if t < 2 else deal_scales
+            deal(t % 2)
         quantize_u(0, 0, J)
-        deal_scales(1)
         for t in range(PACK):
             first_product(0, t, 0, J)
 
@@ -150,10 +156,11 @@ def tile_list_offsetpicks_peakgated_rowabove_kernel(tc, xf, ow, fk, w_words, w_s
                 step(1, PACK - 1, j0, j1)
         for j0, j1 in halves:
             quantize_u(1, j0, j1)
-        for t0 in (0, 2):
-            for j0, j1 in halves:
-                for t in (t0, t0 + 1):
-                    first_product(1, t, j0, j1)
+        for j0, j1 in halves:
+            for t in (0, 1):
+                first_product(1, t, j0, j1)
+        for t in (2, 3):
+            first_product(1, t, 0, J)
 
         neg_peak = [keep.tile([P, 1], F32, name="neg_peak_%d" % t) for t in range(PACK)]
         above = keep.tile([P, PACK, J], F32, name="above")

@@ -24,6 +24,7 @@ PACK = 4
 PASSES = K // (P * PACK)
 HALF = J // 2
 LIST_COL = 16
+LAST_PASS_ORDER = (2, 0, 1, 3)
 
 
 def tile_list_offsetpicks_peakgated_rowabove_kernel(tc, xf, ow, fk, w_words, w_scales, wb_words, wb_scales, rs, offs, out):
@@ -33,7 +34,7 @@ def tile_list_offsetpicks_peakgated_rowabove_kernel(tc, xf, ow, fk, w_words, w_s
         psum = ctx.enter_context(tc.psum_pool(name="psum", bufs=1))
 
         offsets = keep.tile([P, J // LIST_COL], U16, name="offsets")
-        tokens = [[keep.tile([P, T], F32, name="tokens_%d_%d" % (z, t)) for t in range(PACK)] for z in range(PASSES)]
+        tokens = [[keep.tile([P, T], F32, name="tokens_%d_%d" % (z, t), align_bytes=64) for t in range(PACK)] for z in range(PASSES)]
         own = [keep.tile([P, PACK, J], F32, name="own_%d" % z) for z in range(PASSES)]
         factor = keep.tile([P, PASSES, PACK], F32, name="factor")
         w_raw = keep.tile([P, PASSES, R // 2], I32, name="w_raw")
@@ -76,7 +77,7 @@ def tile_list_offsetpicks_peakgated_rowabove_kernel(tc, xf, ow, fk, w_words, w_s
         load_w_scale_rows(3)
         load_tokens(0, 3)
         nc.sync.dma_start(out=own[1][:], in_=ow_rows[1])
-        for t in range(PACK):
+        for t in LAST_PASS_ORDER:
             load_tokens(1, t)
         for q in range(4):
             nc.sync.dma_start(
@@ -93,7 +94,7 @@ def tile_list_offsetpicks_peakgated_rowabove_kernel(tc, xf, ow, fk, w_words, w_s
 
         diff = [[keep.tile([P, J], F32, name="diff_%d_%d" % (z, t)) for t in range(PACK)] for z in range(PASSES)]
         u = [keep.tile([P, J, PACK], BF16, name="u_%d" % z, align_bytes=64) for z in range(PASSES)]
-        u_codes = [keep.tile([P, J], U32, name="u_codes_%d" % z, align_bytes=64) for z in range(PASSES)]
+        u_codes = [None, keep.tile([P, J], U32, name="u_codes_1", align_bytes=64)]
         u_plane = [keep.tile([P, J], U8, name="u_plane_%d" % z, align_bytes=64) for z in range(PASSES)]
         first = [psum.tile([P, J], F32, name="first_%d" % t) for t in range(PACK)]
         second = [psum.tile([P, N], F32, name="second_%d" % h) for h in range(2)]
@@ -143,13 +144,14 @@ def tile_list_offsetpicks_peakgated_rowabove_kernel(tc, xf, ow, fk, w_words, w_s
             scale(0, t, 0, J)
             deal = deal_words if t < 2 else deal_scales
             deal(t % 2)
+
+        for t in LAST_PASS_ORDER[:-1]:
+            gather(1, t, 0, J)
+            scale(1, t, 0, J)
+        u_codes[0] = keep.tile([P, J], U32, name="tokens_1_1", align_bytes=64)
         quantize_u(0, 0, J)
         for t in range(PACK):
             first_product(0, t, 0, J)
-
-        for t in range(PACK - 1):
-            gather(1, t, 0, J)
-            scale(1, t, 0, J)
         halves = [(0, HALF), (HALF, J)]
         for step in (gather, scale):
             for j0, j1 in halves:
@@ -200,12 +202,12 @@ def tile_list_offsetpicks_peakgated_rowabove_kernel(tc, xf, ow, fk, w_words, w_s
 
         magnitude = [keep.tile([P, N], BF16, name="magnitude_%d" % h) for h in range(2)]
         mean = [keep.tile([P, 1], F32, name="mean_%d" % h) for h in range(2)]
-        kept = [keep.tile([P, N], F32, name="kept_%d" % h) for h in range(2)]
+        offset = [keep.tile([P, N], F32, name="offset_%d" % h) for h in range(2)]
         result = [keep.tile([P, N], F32, name="result_%d" % h) for h in range(2)]
         for h in range(2):
             nc.scalar.activation(magnitude[h][:], second[h][:], ACT.Abs, scale=1.0 / N, accum_out=mean[h][:])
         for h in range(2):
-            nc.vector.tensor_scalar(kept[h][:], second[h][:], mean[h][:], 0.0, ALU.subtract, ALU.max)
+            nc.vector.tensor_scalar(offset[h][:], resid[:, h, :], -0.3, mean[h][:], ALU.mult, ALU.subtract)
         for h in range(2):
-            nc.vector.scalar_tensor_tensor(result[h][:], resid[:, h, :], -0.3, kept[h][:], ALU.mult, ALU.add)
+            nc.vector.scalar_tensor_tensor(result[h][:], second[h][:], mean[h][:], offset[h][:], ALU.max, ALU.add)
             nc.sync.dma_start(out=out[HALF * h : HALF * (h + 1), :], in_=result[h][:])

@@ -24,6 +24,7 @@ PACK = 4
 PASSES = K // (P * PACK)
 HALF = J // 2
 LIST_COL = 16
+FACTOR_ROW = 16
 LAST_PASS_ORDER = (2, 0, 1, 3)
 
 
@@ -67,7 +68,7 @@ def tile_list_offsetpicks_peakgated_rowabove_kernel(tc, xf, ow, fk, w_words, w_s
         load_tokens(0, 0)
         nc.sync.dma_start(offsets[:], offs)
         nc.sync.dma_start(out=own[0][:], in_=ow_rows[0])
-        nc.sync.dma_start(out=factor_rows[0:PASSES, :], in_=fk.rearrange("(z c) o -> z (c o)", z=PASSES))
+        nc.sync.dma_start(out=factor_rows[FACTOR_ROW : FACTOR_ROW + PASSES, :], in_=fk.rearrange("(z c) o -> z (c o)", z=PASSES))
         nc.sync.dma_start(out=w_raw[:], in_=w_words.rearrange("z p c -> p z c").bitcast(I32))
         load_tokens(0, 1)
         load_w_scale_rows(0)
@@ -90,7 +91,7 @@ def tile_list_offsetpicks_peakgated_rowabove_kernel(tc, xf, ow, fk, w_words, w_s
         turned = psum.tile([P, PACK, P], F32, name="turned")
         for t in range(PACK):
             nc.tensor.transpose(turned[:, t, :], factor_rows[:, t :: PACK], identity[:])
-        nc.scalar.copy(factor[:], turned[:, :, 0:PASSES].rearrange("p t z -> p z t"))
+        nc.scalar.copy(factor[:], turned[:, :, FACTOR_ROW : FACTOR_ROW + PASSES].rearrange("p t z -> p z t"))
 
         diff = [[keep.tile([P, J], F32, name="diff_%d_%d" % (z, t)) for t in range(PACK)] for z in range(PASSES)]
         u = [keep.tile([P, J, PACK], BF16, name="u_%d" % z, align_bytes=64) for z in range(PASSES)]
@@ -145,13 +146,15 @@ def tile_list_offsetpicks_peakgated_rowabove_kernel(tc, xf, ow, fk, w_words, w_s
             deal = deal_words if t < 2 else deal_scales
             deal(t % 2)
 
-        for t in LAST_PASS_ORDER[:-1]:
+        for t in LAST_PASS_ORDER[:2]:
             gather(1, t, 0, J)
             scale(1, t, 0, J)
-        u_codes[0] = keep.tile([P, J], U32, name="tokens_1_1", align_bytes=64)
+        u_codes[0] = keep.tile([P, J], U32, name="tokens_1_0", align_bytes=64)
         quantize_u(0, 0, J)
         for t in range(PACK):
             first_product(0, t, 0, J)
+        gather(1, LAST_PASS_ORDER[2], 0, J)
+        scale(1, LAST_PASS_ORDER[2], 0, J)
         halves = [(0, HALF), (HALF, J)]
         for step in (gather, scale):
             for j0, j1 in halves:

from contextlib import ExitStack

import concourse.mybir as mybir
from concourse.masks import make_identity

K, T, J, R, N = 1024, 1024, 256, 512, 256
FLOPS = 2 * K * R * J + 2 * R * J * N

F32 = mybir.dt.float32
BF16 = mybir.dt.bfloat16
I32 = mybir.dt.int32
U32 = mybir.dt.uint32
U16 = mybir.dt.uint16
U8 = mybir.dt.uint8
E4M3X4 = mybir.dt.float8_e4m3fn_x4
E5M2X4 = mybir.dt.float8_e5m2_x4
E2M1X4 = mybir.dt.float4_e2m1fn_x4
ALU = mybir.AluOpType
ACT = mybir.ActivationFunctionType
AXIS_X = mybir.AxisListType.X

P = 128
PACK = 4
PASSES = K // (P * PACK)
HALF = J // 2
LIST_COL = 16
FACTOR_ROW = 16
LAST_PASS_ORDER = (2, 0, 1, 3)


def tile_list_offsetpicks_peakgated_rowabove_kernel(tc, xf, ow, fk, w_words, w_scales, wb_words, wb_scales, rs, offs, out):
    nc = tc.nc
    with ExitStack() as ctx:
        keep = ctx.enter_context(tc.tile_pool(name="keep", bufs=1))
        psum = ctx.enter_context(tc.psum_pool(name="psum", bufs=1))

        offsets = keep.tile([P, J // LIST_COL], U16, name="offsets")
        tokens = [[keep.tile([P, T], F32, name="tokens_%d_%d" % (z, t), align_bytes=64) for t in range(PACK)] for z in range(PASSES)]
        own = [keep.tile([P, PACK, J], F32, name="own_%d" % z) for z in range(PASSES)]
        factor = keep.tile([P, PASSES, PACK], F32, name="factor")
        w_raw = keep.tile([P, PASSES, R // 2], I32, name="w_raw")
        w_codes = keep.tile([P, PASSES, R], U16, name="w_codes", align_bytes=64)
        ws_raw = keep.tile([P, PASSES, R], U8, name="ws_raw")
        w_plane = keep.tile([P, PASSES, R], U8, name="w_plane", align_bytes=64)
        wb_codes = keep.tile([P, N], I32, name="wb_codes", align_bytes=64)
        wb_plane = keep.tile([P, N], U8, name="wb_plane", align_bytes=64)
        resid = keep.tile([P, 2, N], F32, name="resid")

        factor_rows = keep.tile([P, P * PACK], F32, name="factor_rows")
        identity = keep.tile([P, P], F32, name="identity")
        nc.gpsimd.memset(factor_rows[:], 0.0)
        nc.gpsimd.memset(ws_raw[:].bitcast(I32), 0)
        make_identity(nc, identity[:])
        nc.gpsimd.memset(wb_plane[:].bitcast(I32), 0)

        xf_rows = xf.rearrange("(z p t) c -> z t p c", z=PASSES, t=PACK)
        ow_rows = ow.rearrange("(z p t) j -> z p t j", z=PASSES, t=PACK)

        def load_tokens(z, t):
            nc.sync.dma_start(out=tokens[z][t][:], in_=xf_rows[z, t])

        def load_w_scale_rows(q):
            nc.sync.dma_start(
                out=ws_raw[32 * q : 32 * q + 4].bitcast(I32),
                in_=w_scales[:, 4 * q : 4 * q + 4, :].rearrange("z q c -> q z c").bitcast(I32),
            )

        load_tokens(0, 0)
        nc.sync.dma_start(offsets[:], offs)
        nc.sync.dma_start(out=own[0][:], in_=ow_rows[0])
        nc.sync.dma_start(out=factor_rows[FACTOR_ROW : FACTOR_ROW + PASSES, :], in_=fk.rearrange("(z c) o -> z (c o)", z=PASSES))
        nc.sync.dma_start(out=w_raw[:], in_=w_words.rearrange("z p c -> p z c").bitcast(I32))
        load_tokens(0, 1)
        load_w_scale_rows(0)
        load_w_scale_rows(1)
        load_tokens(0, 2)
        load_w_scale_rows(2)
        load_w_scale_rows(3)
        load_tokens(0, 3)
        nc.sync.dma_start(out=own[1][:], in_=ow_rows[1])
        for t in LAST_PASS_ORDER:
            load_tokens(1, t)
        for q in range(4):
            nc.sync.dma_start(
                out=wb_plane[32 * q : 32 * q + 4].bitcast(I32),
                in_=wb_scales[0, 4 * q : 4 * q + 4, :].bitcast(I32),
            )
        nc.sync.dma_start(out=wb_codes[:], in_=wb_words[0].rearrange("p n t -> p (n t)").bitcast(I32))
        nc.sync.dma_start(out=resid[:], in_=rs.rearrange("(h p) n -> p h n", h=2))

        turned = psum.tile([P, PACK, P], F32, name="turned")
        for t in range(PACK):
            nc.tensor.transpose(turned[:, t, :], factor_rows[:, t :: PACK], identity[:])
        nc.scalar.copy(factor[:], turned[:, :, FACTOR_ROW : FACTOR_ROW + PASSES].rearrange("p t z -> p z t"))

        diff = [[keep.tile([P, J], F32, name="diff_%d_%d" % (z, t)) for t in range(PACK)] for z in range(PASSES)]
        u = [keep.tile([P, J, PACK], BF16, name="u_%d" % z, align_bytes=64) for z in range(PASSES)]
        u_codes = [None, keep.tile([P, J], U32, name="u_codes_1", align_bytes=64)]
        u_plane = [keep.tile([P, J], U8, name="u_plane_%d" % z, align_bytes=64) for z in range(PASSES)]
        first = [psum.tile([P, J], F32, name="first_%d" % t) for t in range(PACK)]
        second = [psum.tile([P, N], F32, name="second_%d" % h) for h in range(2)]

        def gather(z, t, j0, j1):
            window = tokens[z][t][:].indirect(offsets[:, j0 // LIST_COL : j1 // LIST_COL])
            nc.vector.tensor_tensor(diff[z][t][:, j0:j1], window, own[z][:, t, j0:j1], ALU.subtract)

        def scale(z, t, j0, j1):
            if z == 0 or t < 2:
                nc.scalar.activation(u[z][:, j0:j1, t], diff[z][t][:, j0:j1], ACT.Copy, scale=factor[:, z, t : t + 1])
            else:
                nc.vector.tensor_scalar(u[z][:, j0:j1, t], diff[z][t][:, j0:j1], factor[:, z, t : t + 1], None, ALU.mult)

        def quantize_u(z, j0, j1):
            nc.vector.quantize_mx(
                out=u_codes[z][:, j0:j1].bitcast(E4M3X4),
                scales=u_plane[z][:, j0:j1],
                in_=u[z][:, j0:j1, :].rearrange("p j t -> p (j t)"),
            )

        def first_product(z, t, j0, j1):
            nc.tensor.matmul_mx(
                out=first[t][:, j0:j1],
                lhsT=w_codes[:, z, P * t : P * (t + 1)].bitcast(E2M1X4),
                lhsT_scale=w_plane[:, z, P * t : P * (t + 1)],
                rhs=u_codes[z][:, j0:j1].bitcast(E4M3X4),
                rhs_scale=u_plane[z][:, j0:j1],
                start=(z == 0),
                stop=(z == PASSES - 1 and j1 == J),
            )

        def deal_words(z):
            nc.vector.tensor_copy(
                w_codes[:, z, :].rearrange("p (t c i) -> p c t i", t=PACK, i=8),
                w_raw[:, z, :].bitcast(U16).rearrange("p (c i t) -> p c t i", t=PACK, i=8),
            )

        def deal_scales(z):
            nc.vector.tensor_copy(
                w_plane[:, z, :].rearrange("p (t c i) -> p c t i", t=PACK, i=16),
                ws_raw[:, z, :].rearrange("p (c i t) -> p c t i", t=PACK, i=16),
            )

        for t in range(PACK):
            gather(0, t, 0, J)
            scale(0, t, 0, J)
            deal = deal_words if t < 2 else deal_scales
            deal(t % 2)

        for t in LAST_PASS_ORDER[:2]:
            gather(1, t, 0, J)
            scale(1, t, 0, J)
        u_codes[0] = keep.tile([P, J], U32, name="tokens_1_0", align_bytes=64)
        quantize_u(0, 0, J)
        for t in range(PACK):
            first_product(0, t, 0, J)
        gather(1, LAST_PASS_ORDER[2], 0, J)
        scale(1, LAST_PASS_ORDER[2], 0, J)
        halves = [(0, HALF), (HALF, J)]
        for step in (gather, scale):
            for j0, j1 in halves:
                step(1, PACK - 1, j0, j1)
        for j0, j1 in halves:
            quantize_u(1, j0, j1)
        for j0, j1 in halves:
            for t in (0, 1):
                first_product(1, t, j0, j1)
        for t in (2, 3):
            first_product(1, t, 0, J)

        neg_peak = [keep.tile([P, 1], F32, name="neg_peak_%d" % t) for t in range(PACK)]
        above = keep.tile([P, PACK, J], F32, name="above")
        hid = keep.tile([P, J, PACK], BF16, name="hid", align_bytes=64)
        hid_codes = keep.tile([P, J], U32, name="hid_codes", align_bytes=64)
        hid_plane = keep.tile([P, J], U8, name="hid_plane", align_bytes=64)

        for t in range(PACK):
            nc.vector.tensor_reduce(neg_peak[t][:], first[t][:], AXIS_X, ALU.max, negate=True)
            for j0, j1 in (halves if t == PACK - 1 else [(0, J)]):
                nc.scalar.activation(above[:, t, j0:j1], first[t][:, j0:j1], ACT.Relu, bias=neg_peak[t][:], scale=2.5)

        def weave(t0, j0, j1):
            nc.vector.tensor_scalar(
                hid[:, j0:j1, t0 : t0 + 2], above[:, t0 : t0 + 2, j0:j1].rearrange("p t j -> p j t"), 0.4, None, ALU.mult
            )

        weave(0, 0, J)
        for j0, j1 in halves:
            weave(2, j0, j1)
        for j0, j1 in halves:
            nc.vector.quantize_mx(
                out=hid_codes[:, j0:j1].bitcast(E5M2X4),
                scales=hid_plane[:, j0:j1],
                in_=hid[:, j0:j1, :].rearrange("p j t -> p (j t)"),
            )
        for h, (j0, j1) in enumerate(halves):
            nc.tensor.matmul_mx(
                out=second[h][:],
                lhsT=hid_codes[:, j0:j1].bitcast(E5M2X4),
                lhsT_scale=hid_plane[:, j0:j1],
                rhs=wb_codes[:].bitcast(E5M2X4),
                rhs_scale=wb_plane[:],
                start=True,
                stop=True,
            )

        magnitude = [keep.tile([P, N], BF16, name="magnitude_%d" % h) for h in range(2)]
        mean = [keep.tile([P, 1], F32, name="mean_%d" % h) for h in range(2)]
        offset = [keep.tile([P, N], F32, name="offset_%d" % h) for h in range(2)]
        result = [keep.tile([P, N], F32, name="result_%d" % h) for h in range(2)]
        for h in range(2):
            nc.scalar.activation(magnitude[h][:], second[h][:], ACT.Abs, scale=1.0 / N, accum_out=mean[h][:])
        for h in range(2):
            nc.vector.tensor_scalar(offset[h][:], resid[:, h, :], -0.3, mean[h][:], ALU.mult, ALU.subtract)
        for h in range(2):
            nc.vector.scalar_tensor_tensor(result[h][:], second[h][:], mean[h][:], offset[h][:], ALU.max, ALU.add)
            nc.sync.dma_start(out=out[HALF * h : HALF * (h + 1), :], in_=result[h][:])
